import numpy as np
import ml_dtypes


def mxq(x, axis, fmt="e4m3"):
    dtype, down = {"e4m3": (ml_dtypes.float8_e4m3fn, 7), "e5m2": (ml_dtypes.float8_e5m2, 14)}[fmt]
    v = np.moveaxis(np.asarray(x, np.float32).astype(ml_dtypes.bfloat16).astype(np.float64), axis, -1)
    blocks = v.reshape(v.shape[:-1] + (-1, 32))
    amax = np.abs(blocks).max(-1, keepdims=True)
    byte = np.maximum(np.where(amax > 0, np.frexp(amax)[1] - 1 + 127, 0) - down, 1)
    scale = np.exp2(byte - 127.0)
    codes = (blocks / scale).astype(np.float32).astype(dtype).astype(np.float64)
    return np.moveaxis((codes * scale).reshape(v.shape), -1, axis)


WIDE = False


def mx_kscale(k):
    if not WIDE:
        return np.ones(k)
    levels = np.array([10, -10, 5, -5, 0])
    if k % 512:
        return np.exp2(np.random.permutation(np.resize(levels, k // 32))).repeat(32)
    a = np.empty((k // 512, 16))
    for p in range(k // 512):
        a[p, :8] = np.random.permutation(np.resize(levels, 8))
        for g in range(8):
            far = levels[np.abs(levels - a[p, g]) >= 10]
            a[p, g + 8] = far[np.random.randint(len(far))]
    return np.exp2(a.ravel()).repeat(32)


def f64(x):
    return np.asarray(x).astype(np.float64)


def striped(idx):
    return np.tile(idx.reshape(-1, 16).T, (8, 1)).astype(np.uint16)


def unstriped(offs):
    return offs[:16].T.reshape(-1).astype(np.int64)


def striped8(idx):
    return np.concatenate([x.reshape(-1, 16).T for x in idx]).astype(np.uint16)


def runs(offs, k):
    lists = np.stack([offs[16 * r : 16 * r + 16].T.reshape(-1) for r in range(8)]).astype(np.int64)
    return lists[np.arange(k) % 512 // 64]


def pack_weight(w):
    k, n = w.shape
    w = f64(np.asarray(w, np.float32).astype(ml_dtypes.bfloat16)).reshape(k // 32, 32, n)
    amax = np.abs(w).max(1)
    byte = np.clip(np.where(amax > 0, np.frexp(amax)[1] - 1 + 127 - 7, 1), 1, 254)
    scaled = (w * np.exp2(127.0 - byte)[:, None, :]).reshape(k, n).astype(np.float32)
    words = np.ascontiguousarray(scaled.reshape(k // 512, 128, 4, n).transpose(0, 1, 3, 2)).astype(ml_dtypes.float8_e4m3fn).view(np.uint8)
    return words, np.ascontiguousarray(byte.astype(np.uint8).reshape(k // 512, 16, n))


def unpack_weight(words, scales):
    g, p, n, _ = words.shape
    vals = np.ascontiguousarray(words).view(ml_dtypes.float8_e4m3fn).astype(np.float64) * np.repeat(np.exp2(scales.astype(np.float64) - 127.0), 8, axis=1)[..., None]
    return vals.transpose(0, 1, 3, 2).reshape(g * 512, n)


def sigmoid(v):
    return 1.0 / (1.0 + np.exp(-np.maximum(v, -700.0)))

def planes(y):
    n, m = y.shape
    v = y.astype(np.float32).astype(ml_dtypes.bfloat16).astype(np.float64).reshape(n // 32, 32, m)
    top = np.abs(v).max(1)
    byte = np.clip(np.where(top > 0, np.frexp(top)[1] - 1 + 127 - 7, 1), 1, 254)
    codes = (v * np.exp2(127.0 - byte)[:, None, :]).reshape(n, m).astype(np.float32).astype(ml_dtypes.float8_e4m3fn).view(np.uint8)
    words = codes.reshape(n // 512, 128, 4, m).transpose(0, 1, 3, 2)
    return np.ascontiguousarray(words), np.ascontiguousarray(byte.astype(np.uint8).reshape(n // 512, 16, m))


K, T, S, H, G = 512, 2048, 512, 512, 2048


def setup_inputs():
    n = np.random.standard_normal
    s = mx_kscale(K)[:, None]
    packed_xT = pack_weight(n((K, T)) * s)
    packed_w1 = pack_weight(n((K, H)) / np.sqrt(K) / s)
    packed_dT = pack_weight(n((K, G)) / s)
    return {
        "x_words": packed_xT[0],
        "x_scales": packed_xT[1],
        "w1_words": packed_w1[0],
        "w1_scales": packed_w1[1],
        "gs": (np.random.uniform(0.5, 1.5, (K, 1)) * s).astype(np.float32),
        "d_words": packed_dT[0],
        "d_scales": packed_dT[1],
        "offs": striped(np.random.permutation(T)[:S]),
        "nb": striped8(np.stack([np.random.permutation(S) for _ in range(8)])),
        "k1": striped8(np.random.randint(0, G, (8, H))),
    }


def reference(x_words, x_scales, w1_words, w1_scales, gs, d_words, d_scales, offs, nb, k1):
    d_k1 = unpack_weight(d_words, d_scales)[np.arange(K)[:, None], runs(k1, K)]
    xq = unpack_weight(x_words, x_scales)[:, unstriped(offs)]
    h = unpack_weight(w1_words, w1_scales).T @ xq
    z = f64(gs) * (np.tanh(h + h[np.arange(H)[:, None], runs(nb, H)]))
    gv = 0.0625 * ((d_k1.T @ mxq(z, 0, "e4m3")))
    out_0 = sigmoid(gv) * h
    return (out_0,) + planes(out_0)

@@ -1,0 +1,186 @@
+from contextlib import ExitStack
+
+import concourse.mybir as mybir
+
+K, T, S, H, G = 512, 2048, 512, 512, 2048
+FLOPS = 2 * K * H * S * 2
+
+F32 = mybir.dt.float32
+BF16 = mybir.dt.bfloat16
+I32 = mybir.dt.int32
+U32 = mybir.dt.uint32
+U16 = mybir.dt.uint16
+U8 = mybir.dt.uint8
+FP8X4 = mybir.dt.float8_e4m3fn_x4
+ADD = mybir.AluOpType.add
+MULT = mybir.AluOpType.mult
+COPY = mybir.ActivationFunctionType.Copy
+TANH = mybir.ActivationFunctionType.Tanh
+
+P = 128
+PACK = 4
+HALF = S // 2
+CHUNK = 128
+CHUNKS = S // CHUNK
+
+
+def deal(nc, dealt, plain, run):
+    nc.vector.tensor_copy(
+        out=dealt[:].rearrange("p (t c i) -> p c t i", t=PACK, i=run),
+        in_=plain[:].rearrange("p (c i t) -> p c t i", t=PACK, i=run),
+    )
+
+
+def tile_picked_densepq_tanh_po_kernel(tc, x_words, x_scales, w1_words, w1_scales, gs, d_words, d_scales, offs, nb, k1, out_0, out_1, out_2):
+    nc = tc.nc
+    with ExitStack() as ctx:
+        keep = ctx.enter_context(tc.tile_pool(name="keep", bufs=1))
+        psum = ctx.enter_context(tc.psum_pool(name="psum", bufs=1))
+
+        offs_t = keep.tile([P, S // 16], U16)
+        nb_t = keep.tile([P, S // 16], U16)
+        k1_t = keep.tile([P, H // 16], U16)
+        x_win = keep.tile([P, T], U32, align_bytes=64)
+        xs_win = keep.tile([P, T], U8, align_bytes=64)
+        ds_win = keep.tile([P, G], U8, align_bytes=64)
+        w_raw = keep.tile([P, H], U32, tag="words", align_bytes=64)
+        ws_raw = keep.tile([P, H], U8, tag="bytes", align_bytes=64)
+        gain = keep.tile([P, PACK], F32)
+        warm = keep.tile([P, 8], F32)
+        warm_out = keep.tile([P, 8], F32)
+
+        nc.vector.memset(xs_win[:].bitcast(I32), 0)
+        nc.gpsimd.memset(warm[:], 0.0)
+        nc.vector.memset(ds_win[:].bitcast(I32), 0)
+        nc.vector.memset(ws_raw[:].bitcast(I32), 0)
+
+        nc.sync.dma_start(offs_t[:], offs)
+        nc.sync.dma_start(w_raw[:].bitcast(I32), w1_words[0].rearrange("p c r -> p (c r)").bitcast(I32))
+        for r in range(4):
+            nc.sync.dma_start(xs_win[r:P:32, :].bitcast(I32), x_scales[0, r:16:4, :].bitcast(I32))
+        nc.sync.dma_start(x_win[:].bitcast(I32), x_words[0].rearrange("p c r -> p (c r)").bitcast(I32))
+        nc.sync.dma_start(k1_t[:], k1)
+        nc.scalar.activation(warm_out[:], warm[:], TANH)
+        for r in range(4):
+            nc.scalar.dma_start(ws_raw[r:P:32, :].bitcast(I32), w1_scales[0, r:16:4, :].bitcast(I32))
+        nc.sync.dma_start(nb_t[:], nb)
+        nc.gpsimd.dma_start(ds_win[0:P:8, :].bitcast(I32), d_scales[0].bitcast(I32))
+        nc.gpsimd.dma_start(gain[:], gs.rearrange("(p t) o -> p (t o)", t=PACK))
+
+        xq = keep.tile([P, S], U32, align_bytes=64)
+        xq_s = keep.tile([P, S], U8, align_bytes=64)
+        w_q = keep.tile([P, H], U32, align_bytes=64)
+        w_s = keep.tile([P, H], U8, align_bytes=64)
+        dq = keep.tile([P, H], U32, align_bytes=64)
+        d_q = keep.tile([P, H], U32, align_bytes=64)
+        d_s = keep.tile([P, H], U8, align_bytes=64)
+
+        nc.vector.tensor_copy(xq_s[:], xs_win[:].indirect(offs_t[:]))
+        deal(nc, w_q, w_raw, 4)
+        deal(nc, w_s, ws_raw, 16)
+        d_win = keep.tile([P, G], U32, tag="words", align_bytes=64)
+        nc.sync.dma_start(d_win[:].bitcast(I32), d_words[0].rearrange("p c r -> p (c r)").bitcast(I32))
+
+        h_bank = [psum.tile([P, S], F32, name="h_bank%d" % t) for t in range(PACK)]
+        for half in range(2):
+            cols = slice(half * HALF, (half + 1) * HALF)
+            nc.vector.tensor_copy(xq[:, cols], x_win[:].indirect(offs_t[:, half * 16 : (half + 1) * 16]))
+            for t in range(PACK):
+                m = slice(t * P, (t + 1) * P)
+                nc.tensor.matmul_mx(
+                    out=h_bank[t][:, cols],
+                    lhsT=w_q[:, m].bitcast(FP8X4),
+                    lhsT_scale=w_s[:, m],
+                    rhs=xq[:, cols].bitcast(FP8X4),
+                    rhs_scale=xq_s[:, cols],
+                    start=True,
+                    stop=True,
+                )
+
+        dq_s = keep.tile([P, H], U8, tag="bytes", align_bytes=64)
+        nc.vector.tensor_copy(dq_s[:], ds_win[:].indirect(k1_t[:]))
+        deal(nc, d_s, dq_s, 16)
+        for r in range(1, 4):
+            nc.sync.dma_start(d_s[r:P:32, :].bitcast(I32), d_s[8 * r : P : 32, :].bitcast(I32))
+        nc.vector.tensor_copy(dq[:], d_win[:].indirect(k1_t[:]))
+        deal(nc, d_q, dq, 4)
+
+        window = [keep.tile([P, S], F32, name="window%d" % t) for t in range(PACK)]
+        own = [keep.tile([P, PACK, HALF], F32, name="own%d" % b) for b in range(2)]
+        pre = [keep.tile([P, PACK, HALF], F32, name="pre%d" % b) for b in range(2)]
+        for t in range(PACK):
+            nc.scalar.activation(window[t][:], h_bank[t][:], COPY, scale=0.5)
+        for t in range(PACK):
+            nc.vector.tensor_copy(own[0][:, t, :], window[t][:, 0:HALF])
+            nc.vector.tensor_tensor(pre[0][:, t, :], window[t][:].indirect(nb_t[:, 0:16]), own[0][:, t, :], ADD)
+        for t in range(PACK):
+            nc.scalar.activation(own[1][:, t, :], h_bank[t][:, HALF:S], COPY, scale=0.5)
+
+        out_rows = out_0.rearrange("(p t) j -> p t j", t=PACK)
+        out_words = out_1[0].rearrange("p c r -> p (c r)").bitcast(I32)
+        o_s = keep.tile([P, S], U8, align_bytes=64)
+        state = {}
+
+        def gather(c):
+            b, lo = divmod(c * CHUNK, HALF)
+            for t in range(PACK):
+                nc.vector.tensor_tensor(
+                    pre[b][:, t, lo : lo + CHUNK],
+                    window[t][:].indirect(nb_t[:, c * 8 : (c + 1) * 8]),
+                    own[b][:, t, lo : lo + CHUNK],
+                    ADD,
+                )
+
+        def hidden(c):
+            b, lo = divmod(c * CHUNK, HALF)
+            th = keep.tile([P, CHUNK, PACK], F32, name="th%d" % c)
+            nc.scalar.activation(th[:], pre[b][:, :, lo : lo + CHUNK].rearrange("p t j -> p j t"), TANH, scale=2.0)
+            z = keep.tile([P, CHUNK, PACK], BF16, name="z%d" % c, align_bytes=64)
+            nc.vector.tensor_tensor(z[:], th[:], gain[:].unsqueeze(1).to_broadcast([P, CHUNK, PACK]), MULT)
+            z_q = keep.tile([P, CHUNK], U32, name="z_q%d" % c, align_bytes=64)
+            z_s = keep.tile([P, CHUNK], U8, name="z_s%d" % c, align_bytes=64)
+            nc.vector.quantize_mx(out=z_q[:].bitcast(FP8X4), scales=z_s[:], in_=z[:].rearrange("p j t -> p (j t)"))
+            bank = psum.tile([P, PACK, CHUNK], F32, name="g_bank%d" % c)
+            for t in range(PACK):
+                m = slice(t * P, (t + 1) * P)
+                nc.tensor.matmul_mx(
+                    out=bank[:, t, :],
+                    lhsT=d_q[:, m].bitcast(FP8X4),
+                    lhsT_scale=d_s[:, m],
+                    rhs=z_q[:].bitcast(FP8X4),
+                    rhs_scale=z_s[:],
+                    start=True,
+                    stop=True,
+                )
+            gate = keep.tile([P, PACK, CHUNK], F32, name="gate%d" % c)
+            nc.scalar.activation(gate[:], bank[:], TANH, scale=0.03125)
+            state[c] = gate
+
+        def finish(c):
+            b, lo = divmod(c * CHUNK, HALF)
+            cols = slice(c * CHUNK, (c + 1) * CHUNK)
+            y = keep.tile([P, PACK, CHUNK], F32, name="y%d" % c)
+            nc.vector.scalar_tensor_tensor(y[:], state[c][:], 1.0, own[b][:, :, lo : lo + CHUNK], ADD, MULT)
+            nc.sync.dma_start(out_rows[:, :, cols], y[:])
+            yb = keep.tile([P, CHUNK, PACK], BF16, name="yb%d" % c, align_bytes=64)
+            nc.scalar.copy(
+                yb[:].rearrange("p (c i) t -> p c t i", i=4),
+                y[:].rearrange("p t (c i) -> p c t i", i=4),
+            )
+            y_q = keep.tile([P, CHUNK], U32, name="y_q%d" % c, align_bytes=64)
+            nc.vector.quantize_mx(out=y_q[:].bitcast(FP8X4), scales=o_s[:, cols], in_=yb[:].rearrange("p j t -> p (j t)"))
+            nc.sync.dma_start(out_words[:, cols], y_q[:].bitcast(I32))
+
+        gather(2)
+        hidden(0)
+        hidden(1)
+        gather(3)
+        finish(0)
+        hidden(2)
+        finish(1)
+        hidden(3)
+        finish(2)
+        finish(3)
+        for r in range(4):
+            queue = nc.sync if r % 2 else nc.scalar
+            queue.dma_start(out_2[0, r:16:4, :].bitcast(I32), o_s[r:P:32, :].bitcast(I32))

@@ -26,8 +26,8 @@ CHUNKS = S // CHUNK
 
 def deal(nc, dealt, plain, run):
     nc.vector.tensor_copy(
-        out=dealt[:].rearrange("p (t c i) -> p c t i", t=PACK, i=run),
-        in_=plain[:].rearrange("p (c i t) -> p c t i", t=PACK, i=run),
+        out=dealt.rearrange("p (t c i) -> p c t i", t=PACK, i=run),
+        in_=plain.rearrange("p (c i t) -> p c t i", t=PACK, i=run),
     )
 
 
@@ -40,103 +40,99 @@ def tile_picked_densepq_tanh_po_kernel(tc, x_words, x_scales, w1_words, w1_scale
         offs_t = keep.tile([P, S // 16], U16)
         nb_t = keep.tile([P, S // 16], U16)
         k1_t = keep.tile([P, H // 16], U16)
-        x_win = keep.tile([P, T], U32, align_bytes=64)
+        x_win = keep.tile([P, T], U32, tag="tokens", align_bytes=64)
         xs_win = keep.tile([P, T], U8, align_bytes=64)
+        d_win = keep.tile([P, G], U32, align_bytes=64)
         ds_win = keep.tile([P, G], U8, align_bytes=64)
-        w_raw = keep.tile([P, H], U32, tag="words", align_bytes=64)
-        ws_raw = keep.tile([P, H], U8, tag="bytes", align_bytes=64)
+        w_raw = keep.tile([P, H], U32, align_bytes=64)
+        ws_raw = keep.tile([P, H], U8, align_bytes=64)
         gain = keep.tile([P, PACK], F32)
         warm = keep.tile([P, 8], F32)
         warm_out = keep.tile([P, 8], F32)
 
-        nc.vector.memset(xs_win[:].bitcast(I32), 0)
-        nc.gpsimd.memset(warm[:], 0.0)
-        nc.vector.memset(ds_win[:].bitcast(I32), 0)
+        nc.gpsimd.memset(ds_win[:].bitcast(I32), 0)
         nc.vector.memset(ws_raw[:].bitcast(I32), 0)
+        nc.vector.memset(xs_win[:].bitcast(I32), 0)
+        nc.vector.memset(warm[:], 0.0)
 
         nc.sync.dma_start(offs_t[:], offs)
-        nc.sync.dma_start(w_raw[:].bitcast(I32), w1_words[0].rearrange("p c r -> p (c r)").bitcast(I32))
-        for r in range(4):
-            nc.sync.dma_start(xs_win[r:P:32, :].bitcast(I32), x_scales[0, r:16:4, :].bitcast(I32))
-        nc.sync.dma_start(x_win[:].bitcast(I32), x_words[0].rearrange("p c r -> p (c r)").bitcast(I32))
         nc.sync.dma_start(k1_t[:], k1)
-        nc.scalar.activation(warm_out[:], warm[:], TANH)
-        for r in range(4):
-            nc.scalar.dma_start(ws_raw[r:P:32, :].bitcast(I32), w1_scales[0, r:16:4, :].bitcast(I32))
+        nc.sync.dma_start(ws_raw[0:P:8, :].bitcast(I32), w1_scales[0].bitcast(I32))
+        nc.sync.dma_start(w_raw[:].bitcast(I32), w1_words[0].rearrange("p c r -> p (c r)").bitcast(I32))
+        nc.sync.dma_start(xs_win[0:P:8, :].bitcast(I32), x_scales[0].bitcast(I32))
+        nc.sync.dma_start(ds_win[0:P:8, :].bitcast(I32), d_scales[0].bitcast(I32))
+        nc.sync.dma_start(x_win[:].bitcast(I32), x_words[0].rearrange("p c r -> p (c r)").bitcast(I32))
+        nc.sync.dma_start(d_win[:].bitcast(I32), d_words[0].rearrange("p c r -> p (c r)").bitcast(I32))
         nc.sync.dma_start(nb_t[:], nb)
-        nc.gpsimd.dma_start(ds_win[0:P:8, :].bitcast(I32), d_scales[0].bitcast(I32))
-        nc.gpsimd.dma_start(gain[:], gs.rearrange("(p t) o -> p (t o)", t=PACK))
+        nc.sync.dma_start(gain[:], gs.rearrange("(p t) o -> p (t o)", t=PACK))
+        nc.scalar.activation(warm_out[:], warm[:], TANH)
 
         xq = keep.tile([P, S], U32, align_bytes=64)
-        xq_s = keep.tile([P, S], U8, align_bytes=64)
+        picked_s = keep.tile([P, S], U8, align_bytes=64)
         w_q = keep.tile([P, H], U32, align_bytes=64)
-        w_s = keep.tile([P, H], U8, align_bytes=64)
+        planes = keep.tile([P, H + S], U8, align_bytes=64)
         dq = keep.tile([P, H], U32, align_bytes=64)
+        dq_s = keep.tile([P, H], U8, align_bytes=64)
         d_q = keep.tile([P, H], U32, align_bytes=64)
-        d_s = keep.tile([P, H], U8, align_bytes=64)
+        w_s = planes[:, 0:H]
+        xq_s = planes[:, H : H + S]
 
-        nc.vector.tensor_copy(xq_s[:], xs_win[:].indirect(offs_t[:]))
-        deal(nc, w_q, w_raw, 4)
-        deal(nc, w_s, ws_raw, 16)
-        d_win = keep.tile([P, G], U32, tag="words", align_bytes=64)
-        nc.sync.dma_start(d_win[:].bitcast(I32), d_words[0].rearrange("p c r -> p (c r)").bitcast(I32))
+        def settle(plane):
+            for r in range(1, 4):
+                nc.scalar.dma_start(plane[r:P:32, :].bitcast(I32), plane[8 * r : P : 32, :].bitcast(I32))
 
-        h_bank = [psum.tile([P, S], F32, name="h_bank%d" % t) for t in range(PACK)]
-        for half in range(2):
-            cols = slice(half * HALF, (half + 1) * HALF)
-            nc.vector.tensor_copy(xq[:, cols], x_win[:].indirect(offs_t[:, half * 16 : (half + 1) * 16]))
-            for t in range(PACK):
-                m = slice(t * P, (t + 1) * P)
-                nc.tensor.matmul_mx(
-                    out=h_bank[t][:, cols],
-                    lhsT=w_q[:, m].bitcast(FP8X4),
-                    lhsT_scale=w_s[:, m],
-                    rhs=xq[:, cols].bitcast(FP8X4),
-                    rhs_scale=xq_s[:, cols],
-                    start=True,
-                    stop=True,
-                )
-
-        dq_s = keep.tile([P, H], U8, tag="bytes", align_bytes=64)
+        deal(nc, w_s, ws_raw[:], 16)
+        nc.vector.tensor_copy(picked_s[:], xs_win[:].indirect(offs_t[:]))
+        nc.vector.tensor_copy(xq_s.bitcast(I32), picked_s[:].bitcast(I32))
+        settle(planes)
+        deal(nc, w_q[:], w_raw[:], 4)
         nc.vector.tensor_copy(dq_s[:], ds_win[:].indirect(k1_t[:]))
-        deal(nc, d_s, dq_s, 16)
-        for r in range(1, 4):
-            nc.sync.dma_start(d_s[r:P:32, :].bitcast(I32), d_s[8 * r : P : 32, :].bitcast(I32))
-        nc.vector.tensor_copy(dq[:], d_win[:].indirect(k1_t[:]))
-        deal(nc, d_q, dq, 4)
+        nc.vector.tensor_copy(xq[:], x_win[:].indirect(offs_t[:]))
+        d_s = keep.tile([P, H], U8, tag="tokens", align_bytes=64)
+        deal(nc, d_s[:], dq_s[:], 16)
+        settle(d_s)
 
         window = [keep.tile([P, S], F32, name="window%d" % t) for t in range(PACK)]
         own = [keep.tile([P, PACK, HALF], F32, name="own%d" % b) for b in range(2)]
         pre = [keep.tile([P, PACK, HALF], F32, name="pre%d" % b) for b in range(2)]
+        h_bank = [psum.tile([P, S], F32, name="h_bank%d" % t) for t in range(PACK)]
         for t in range(PACK):
-            nc.scalar.activation(window[t][:], h_bank[t][:], COPY, scale=0.5)
-        for t in range(PACK):
-            nc.vector.tensor_copy(own[0][:, t, :], window[t][:, 0:HALF])
-            nc.vector.tensor_tensor(pre[0][:, t, :], window[t][:].indirect(nb_t[:, 0:16]), own[0][:, t, :], ADD)
-        for t in range(PACK):
-            nc.scalar.activation(own[1][:, t, :], h_bank[t][:, HALF:S], COPY, scale=0.5)
+            m = slice(t * P, (t + 1) * P)
+            nc.tensor.matmul_mx(
+                out=h_bank[t][:],
+                lhsT=w_q[:, m].bitcast(FP8X4),
+                lhsT_scale=w_s[:, m],
+                rhs=xq[:].bitcast(FP8X4),
+                rhs_scale=xq_s,
+                start=True,
+                stop=True,
+            )
+
+        nc.vector.tensor_copy(dq[:], d_win[:].indirect(k1_t[:]))
+        deal(nc, d_q[:], dq[:], 4)
+
+        def to_own(b, t):
+            nc.scalar.activation(own[b][:, t, :], h_bank[t][:, b * HALF : (b + 1) * HALF], COPY, scale=0.5)
+
+        def gather(b, t):
+            nc.vector.tensor_tensor(
+                pre[b][:, t, :], window[t][:].indirect(nb_t[:, b * 16 : (b + 1) * 16]), own[b][:, t, :], ADD
+            )
 
         out_rows = out_0.rearrange("(p t) j -> p t j", t=PACK)
         out_words = out_1[0].rearrange("p c r -> p (c r)").bitcast(I32)
         o_s = keep.tile([P, S], U8, align_bytes=64)
-        state = {}
+        th = [keep.tile([P, CHUNK, PACK], F32, name="th%d" % c) for c in range(CHUNKS)]
+        gate = [keep.tile([P, PACK, CHUNK], F32, name="gate%d" % c) for c in range(CHUNKS)]
+        yb = [keep.tile([P, CHUNK, PACK], BF16, name="yb%d" % c, align_bytes=64) for c in range(CHUNKS)]
 
-        def gather(c):
+        def squash(c):
             b, lo = divmod(c * CHUNK, HALF)
-            for t in range(PACK):
-                nc.vector.tensor_tensor(
-                    pre[b][:, t, lo : lo + CHUNK],
-                    window[t][:].indirect(nb_t[:, c * 8 : (c + 1) * 8]),
-                    own[b][:, t, lo : lo + CHUNK],
-                    ADD,
-                )
+            nc.scalar.activation(th[c][:], pre[b][:, :, lo : lo + CHUNK].rearrange("p t j -> p j t"), TANH, scale=2.0)
 
         def hidden(c):
-            b, lo = divmod(c * CHUNK, HALF)
-            th = keep.tile([P, CHUNK, PACK], F32, name="th%d" % c)
-            nc.scalar.activation(th[:], pre[b][:, :, lo : lo + CHUNK].rearrange("p t j -> p j t"), TANH, scale=2.0)
             z = keep.tile([P, CHUNK, PACK], BF16, name="z%d" % c, align_bytes=64)
-            nc.vector.tensor_tensor(z[:], th[:], gain[:].unsqueeze(1).to_broadcast([P, CHUNK, PACK]), MULT)
+            nc.vector.tensor_tensor(z[:], th[c][:], gain[:].unsqueeze(1).to_broadcast([P, CHUNK, PACK]), MULT)
             z_q = keep.tile([P, CHUNK], U32, name="z_q%d" % c, align_bytes=64)
             z_s = keep.tile([P, CHUNK], U8, name="z_s%d" % c, align_bytes=64)
             nc.vector.quantize_mx(out=z_q[:].bitcast(FP8X4), scales=z_s[:], in_=z[:].rearrange("p j t -> p (j t)"))
@@ -152,35 +148,55 @@ def tile_picked_densepq_tanh_po_kernel(tc, x_words, x_scales, w1_words, w1_scale
                     start=True,
                     stop=True,
                 )
-            gate = keep.tile([P, PACK, CHUNK], F32, name="gate%d" % c)
-            nc.scalar.activation(gate[:], bank[:], TANH, scale=0.03125)
-            state[c] = gate
+            nc.scalar.activation(gate[c][:], bank[:], TANH, scale=0.03125)
 
         def finish(c):
             b, lo = divmod(c * CHUNK, HALF)
             cols = slice(c * CHUNK, (c + 1) * CHUNK)
             y = keep.tile([P, PACK, CHUNK], F32, name="y%d" % c)
-            nc.vector.scalar_tensor_tensor(y[:], state[c][:], 1.0, own[b][:, :, lo : lo + CHUNK], ADD, MULT)
+            nc.vector.scalar_tensor_tensor(y[:], gate[c][:], 1.0, own[b][:, :, lo : lo + CHUNK], ADD, MULT)
             nc.sync.dma_start(out_rows[:, :, cols], y[:])
-            yb = keep.tile([P, CHUNK, PACK], BF16, name="yb%d" % c, align_bytes=64)
-            nc.scalar.copy(
-                yb[:].rearrange("p (c i) t -> p c t i", i=4),
-                y[:].rearrange("p t (c i) -> p c t i", i=4),
-            )
+            woven = yb[c][:].rearrange("p (c i) t -> p c t i", i=4)
+            plain = y[:].rearrange("p t (c i) -> p c t i", i=4)
+            if c == CHUNKS - 1:
+                nc.vector.tensor_copy(woven, plain)
+            else:
+                nc.scalar.copy(woven, plain)
+
+        def emit(c):
+            cols = slice(c * CHUNK, (c + 1) * CHUNK)
             y_q = keep.tile([P, CHUNK], U32, name="y_q%d" % c, align_bytes=64)
-            nc.vector.quantize_mx(out=y_q[:].bitcast(FP8X4), scales=o_s[:, cols], in_=yb[:].rearrange("p j t -> p (j t)"))
+            nc.vector.quantize_mx(out=y_q[:].bitcast(FP8X4), scales=o_s[:, cols], in_=yb[c][:].rearrange("p j t -> p (j t)"))
             nc.sync.dma_start(out_words[:, cols], y_q[:].bitcast(I32))
 
-        gather(2)
+        for t in range(PACK):
+            nc.scalar.activation(window[t][:], h_bank[t][:], COPY, scale=0.5)
+            to_own(0, t)
+            gather(0, t)
+        to_own(1, 0)
+        to_own(1, 1)
+        squash(0)
+        gather(1, 0)
+        gather(1, 1)
+        to_own(1, 2)
+        to_own(1, 3)
+        squash(1)
         hidden(0)
+        gather(1, 2)
+        gather(1, 3)
         hidden(1)
-        gather(3)
+        squash(2)
+        squash(3)
         finish(0)
         hidden(2)
-        finish(1)
         hidden(3)
+        finish(1)
+        emit(0)
         finish(2)
+        emit(1)
         finish(3)
+        emit(2)
+        emit(3)
         for r in range(4):
             queue = nc.sync if r % 2 else nc.scalar
             queue.dma_start(out_2[0, r:16:4, :].bitcast(I32), o_s[r:P:32, :].bitcast(I32))

@@ -111,8 +111,6 @@ def tile_picked_densepq_tanh_po_kernel(tc, x_words, x_scales, w1_words, w1_scale
         nc.vector.tensor_copy(dq[:], d_win[:].indirect(k1_t[:]))
         deal(nc, d_q[:], dq[:], 4)
 
-        def to_own(b, t):
-            nc.scalar.activation(own[b][:, t, :], h_bank[t][:, b * HALF : (b + 1) * HALF], COPY, scale=0.5)
 
         def gather(b, t):
             nc.vector.tensor_tensor(
@@ -122,20 +120,21 @@ def tile_picked_densepq_tanh_po_kernel(tc, x_words, x_scales, w1_words, w1_scale
         out_rows = out_0.rearrange("(p t) j -> p t j", t=PACK)
         out_words = out_1[0].rearrange("p c r -> p (c r)").bitcast(I32)
         o_s = keep.tile([P, S], U8, align_bytes=64)
-        th = [keep.tile([P, CHUNK, PACK], F32, name="th%d" % c) for c in range(CHUNKS)]
         gate = [keep.tile([P, PACK, CHUNK], F32, name="gate%d" % c) for c in range(CHUNKS)]
-        yb = [keep.tile([P, CHUNK, PACK], BF16, name="yb%d" % c, align_bytes=64) for c in range(CHUNKS)]
+        z = keep.tile([P, S, PACK], BF16, align_bytes=64)
+        z_q = keep.tile([P, S], U32, align_bytes=64)
+        z_s = keep.tile([P, S], U8, align_bytes=64)
+        yb = keep.tile([P, S, PACK], BF16, align_bytes=64)
+        y_q = keep.tile([P, S], U32, align_bytes=64)
+        y = [keep.tile([P, PACK, CHUNK], F32, name="y%d" % c) for c in range(CHUNKS)]
 
-        def squash(c):
-            b, lo = divmod(c * CHUNK, HALF)
-            nc.scalar.activation(th[c][:], pre[b][:, :, lo : lo + CHUNK].rearrange("p t j -> p j t"), TANH, scale=2.0)
+        def quantize(codes, scales, values, cols):
+            nc.vector.quantize_mx(
+                out=codes[:, cols].bitcast(FP8X4), scales=scales[:, cols], in_=values[:, cols, :].rearrange("p j t -> p (j t)")
+            )
 
-        def hidden(c):
-            z = keep.tile([P, CHUNK, PACK], BF16, name="z%d" % c, align_bytes=64)
-            nc.vector.tensor_tensor(z[:], th[c][:], gain[:].unsqueeze(1).to_broadcast([P, CHUNK, PACK]), MULT)
-            z_q = keep.tile([P, CHUNK], U32, name="z_q%d" % c, align_bytes=64)
-            z_s = keep.tile([P, CHUNK], U8, name="z_s%d" % c, align_bytes=64)
-            nc.vector.quantize_mx(out=z_q[:].bitcast(FP8X4), scales=z_s[:], in_=z[:].rearrange("p j t -> p (j t)"))
+        def second(c):
+            cols = slice(c * CHUNK, (c + 1) * CHUNK)
             bank = psum.tile([P, PACK, CHUNK], F32, name="g_bank%d" % c)
             for t in range(PACK):
                 m = slice(t * P, (t + 1) * P)
@@ -143,8 +142,8 @@ def tile_picked_densepq_tanh_po_kernel(tc, x_words, x_scales, w1_words, w1_scale
                     out=bank[:, t, :],
                     lhsT=d_q[:, m].bitcast(FP8X4),
                     lhsT_scale=d_s[:, m],
-                    rhs=z_q[:].bitcast(FP8X4),
-                    rhs_scale=z_s[:],
+                    rhs=z_q[:, cols].bitcast(FP8X4),
+                    rhs_scale=z_s[:, cols],
                     start=True,
                     stop=True,
                 )
@@ -153,50 +152,51 @@ def tile_picked_densepq_tanh_po_kernel(tc, x_words, x_scales, w1_words, w1_scale
         def finish(c):
             b, lo = divmod(c * CHUNK, HALF)
             cols = slice(c * CHUNK, (c + 1) * CHUNK)
-            y = keep.tile([P, PACK, CHUNK], F32, name="y%d" % c)
-            nc.vector.scalar_tensor_tensor(y[:], gate[c][:], 1.0, own[b][:, :, lo : lo + CHUNK], ADD, MULT)
-            nc.sync.dma_start(out_rows[:, :, cols], y[:])
-            woven = yb[c][:].rearrange("p (c i) t -> p c t i", i=4)
-            plain = y[:].rearrange("p t (c i) -> p c t i", i=4)
-            if c == CHUNKS - 1:
-                nc.vector.tensor_copy(woven, plain)
-            else:
-                nc.scalar.copy(woven, plain)
+            nc.vector.scalar_tensor_tensor(y[c][:], gate[c][:], 1.0, own[b][:, :, lo : lo + CHUNK], ADD, MULT)
+            nc.sync.dma_start(out_rows[:, :, cols], y[c][:])
 
-        def emit(c):
-            cols = slice(c * CHUNK, (c + 1) * CHUNK)
-            y_q = keep.tile([P, CHUNK], U32, name="y_q%d" % c, align_bytes=64)
-            nc.vector.quantize_mx(out=y_q[:].bitcast(FP8X4), scales=o_s[:, cols], in_=yb[c][:].rearrange("p j t -> p (j t)"))
-            nc.sync.dma_start(out_words[:, cols], y_q[:].bitcast(I32))
+        def weave(c, copy):
+            copy(yb[:, c * CHUNK : (c + 1) * CHUNK, :], y[c][:].rearrange("p t j -> p j t"))
+
+        def emit(b):
+            cols = slice(b * HALF, (b + 1) * HALF)
+            quantize(y_q, o_s, yb, cols)
+            nc.sync.dma_start(out_words[:, cols], y_q[:, cols].bitcast(I32))
 
         for t in range(PACK):
             nc.scalar.activation(window[t][:], h_bank[t][:], COPY, scale=0.5)
-            to_own(0, t)
+            nc.scalar.activation(own[0][:, t, :], h_bank[t][:, 0:HALF], COPY, scale=0.5)
+            nc.sync.dma_start(own[1][:, t, :], window[t][:, HALF:S])
             gather(0, t)
-        to_own(1, 0)
-        to_own(1, 1)
-        squash(0)
-        gather(1, 0)
-        gather(1, 1)
-        to_own(1, 2)
-        to_own(1, 3)
-        squash(1)
-        hidden(0)
-        gather(1, 2)
-        gather(1, 3)
-        hidden(1)
-        squash(2)
-        squash(3)
-        finish(0)
-        hidden(2)
-        hidden(3)
-        finish(1)
+        first_th = keep.tile([P, PACK, HALF], F32)
+        first_z = keep.tile([P, PACK, HALF], BF16)
+        nc.scalar.activation(first_th[:], pre[0][:], TANH, scale=2.0)
+        for t in range(PACK):
+            gather(1, t)
+            nc.scalar.activation(first_z[:, t, :], first_th[:, t, :], COPY, scale=gain[:, t : t + 1])
+        nc.vector.tensor_copy(z[:, 0:HALF, :], first_z[:].rearrange("p t j -> p j t"))
+        quantize(z_q, z_s, z, slice(0, HALF))
+        th = [keep.tile([P, CHUNK, PACK], F32, name="th%d" % u) for u in range(2)]
+        for u in range(2):
+            sums = pre[1][:, :, u * CHUNK : (u + 1) * CHUNK]
+            nc.scalar.activation(th[u][:], sums.rearrange("p t j -> p j t"), TANH, scale=2.0)
+        for u in range(2):
+            cols = slice(HALF + u * CHUNK, HALF + (u + 1) * CHUNK)
+            nc.vector.tensor_tensor(z[:, cols, :], th[u][:], gain[:].unsqueeze(1).to_broadcast([P, CHUNK, PACK]), MULT)
+        second(0)
+        second(1)
+        for u in range(2):
+            quantize(z_q, z_s, z, slice(HALF + u * CHUNK, HALF + (u + 1) * CHUNK))
+        second(2)
+        second(3)
+        for c in range(CHUNKS):
+            finish(c)
+        weave(0, nc.scalar.copy)
+        weave(1, nc.scalar.copy)
+        weave(2, nc.vector.tensor_copy)
+        weave(3, nc.vector.tensor_copy)
         emit(0)
-        finish(2)
         emit(1)
-        finish(3)
-        emit(2)
-        emit(3)
         for r in range(4):
             queue = nc.sync if r % 2 else nc.scalar
             queue.dma_start(out_2[0, r:16:4, :].bitcast(I32), o_s[r:P:32, :].bitcast(I32))

from contextlib import ExitStack

import concourse.mybir as mybir

K, T, S, H, G = 512, 2048, 512, 512, 2048
FLOPS = 2 * K * H * S * 2

F32 = mybir.dt.float32
BF16 = mybir.dt.bfloat16
I32 = mybir.dt.int32
U32 = mybir.dt.uint32
U16 = mybir.dt.uint16
U8 = mybir.dt.uint8
FP8X4 = mybir.dt.float8_e4m3fn_x4
ADD = mybir.AluOpType.add
MULT = mybir.AluOpType.mult
COPY = mybir.ActivationFunctionType.Copy
TANH = mybir.ActivationFunctionType.Tanh

P = 128
PACK = 4
HALF = S // 2
CHUNK = 128
CHUNKS = S // CHUNK


def deal(nc, dealt, plain, run):
    nc.vector.tensor_copy(
        out=dealt.rearrange("p (t c i) -> p c t i", t=PACK, i=run),
        in_=plain.rearrange("p (c i t) -> p c t i", t=PACK, i=run),
    )


def tile_picked_densepq_tanh_po_kernel(tc, x_words, x_scales, w1_words, w1_scales, gs, d_words, d_scales, offs, nb, k1, out_0, out_1, out_2):
    nc = tc.nc
    with ExitStack() as ctx:
        keep = ctx.enter_context(tc.tile_pool(name="keep", bufs=1))
        psum = ctx.enter_context(tc.psum_pool(name="psum", bufs=1))

        offs_t = keep.tile([P, S // 16], U16)
        nb_t = keep.tile([P, S // 16], U16)
        k1_t = keep.tile([P, H // 16], U16)
        x_win = keep.tile([P, T], U32, tag="tokens", align_bytes=64)
        xs_win = keep.tile([P, T], U8, align_bytes=64)
        d_win = keep.tile([P, G], U32, align_bytes=64)
        ds_win = keep.tile([P, G], U8, align_bytes=64)
        w_raw = keep.tile([P, H], U32, align_bytes=64)
        ws_raw = keep.tile([P, H], U8, align_bytes=64)
        gain = keep.tile([P, PACK], F32)
        warm = keep.tile([P, 8], F32)
        warm_out = keep.tile([P, 8], F32)

        nc.gpsimd.memset(ds_win[:].bitcast(I32), 0)
        nc.vector.memset(ws_raw[:].bitcast(I32), 0)
        nc.vector.memset(xs_win[:].bitcast(I32), 0)
        nc.vector.memset(warm[:], 0.0)

        nc.sync.dma_start(offs_t[:], offs)
        nc.sync.dma_start(k1_t[:], k1)
        nc.sync.dma_start(ws_raw[0:P:8, :].bitcast(I32), w1_scales[0].bitcast(I32))
        nc.sync.dma_start(w_raw[:].bitcast(I32), w1_words[0].rearrange("p c r -> p (c r)").bitcast(I32))
        nc.sync.dma_start(xs_win[0:P:8, :].bitcast(I32), x_scales[0].bitcast(I32))
        nc.sync.dma_start(ds_win[0:P:8, :].bitcast(I32), d_scales[0].bitcast(I32))
        nc.sync.dma_start(x_win[:].bitcast(I32), x_words[0].rearrange("p c r -> p (c r)").bitcast(I32))
        nc.sync.dma_start(d_win[:].bitcast(I32), d_words[0].rearrange("p c r -> p (c r)").bitcast(I32))
        nc.sync.dma_start(nb_t[:], nb)
        nc.sync.dma_start(gain[:], gs.rearrange("(p t) o -> p (t o)", t=PACK))
        nc.scalar.activation(warm_out[:], warm[:], TANH)

        xq = keep.tile([P, S], U32, align_bytes=64)
        picked_s = keep.tile([P, S], U8, align_bytes=64)
        w_q = keep.tile([P, H], U32, align_bytes=64)
        planes = keep.tile([P, H + S], U8, align_bytes=64)
        dq = keep.tile([P, H], U32, align_bytes=64)
        dq_s = keep.tile([P, H], U8, align_bytes=64)
        d_q = keep.tile([P, H], U32, align_bytes=64)
        w_s = planes[:, 0:H]
        xq_s = planes[:, H : H + S]

        def settle(plane):
            for r in range(1, 4):
                nc.scalar.dma_start(plane[r:P:32, :].bitcast(I32), plane[8 * r : P : 32, :].bitcast(I32))

        deal(nc, w_s, ws_raw[:], 16)
        nc.vector.tensor_copy(picked_s[:], xs_win[:].indirect(offs_t[:]))
        nc.vector.tensor_copy(xq_s.bitcast(I32), picked_s[:].bitcast(I32))
        settle(planes)
        deal(nc, w_q[:], w_raw[:], 4)
        nc.vector.tensor_copy(dq_s[:], ds_win[:].indirect(k1_t[:]))
        nc.vector.tensor_copy(xq[:], x_win[:].indirect(offs_t[:]))
        d_s = keep.tile([P, H], U8, tag="tokens", align_bytes=64)
        deal(nc, d_s[:], dq_s[:], 16)
        settle(d_s)

        window = [keep.tile([P, S], F32, name="window%d" % t) for t in range(PACK)]
        own = [keep.tile([P, PACK, HALF], F32, name="own%d" % b) for b in range(2)]
        pre = [keep.tile([P, PACK, HALF], F32, name="pre%d" % b) for b in range(2)]
        h_bank = [psum.tile([P, S], F32, name="h_bank%d" % t) for t in range(PACK)]
        for t in range(PACK):
            m = slice(t * P, (t + 1) * P)
            nc.tensor.matmul_mx(
                out=h_bank[t][:],
                lhsT=w_q[:, m].bitcast(FP8X4),
                lhsT_scale=w_s[:, m],
                rhs=xq[:].bitcast(FP8X4),
                rhs_scale=xq_s,
                start=True,
                stop=True,
            )

        nc.vector.tensor_copy(dq[:], d_win[:].indirect(k1_t[:]))
        deal(nc, d_q[:], dq[:], 4)


        def gather(b, t):
            nc.vector.tensor_tensor(
                pre[b][:, t, :], window[t][:].indirect(nb_t[:, b * 16 : (b + 1) * 16]), own[b][:, t, :], ADD
            )

        out_rows = out_0.rearrange("(p t) j -> p t j", t=PACK)
        out_words = out_1[0].rearrange("p c r -> p (c r)").bitcast(I32)
        o_s = keep.tile([P, S], U8, align_bytes=64)
        gate = [keep.tile([P, PACK, CHUNK], F32, name="gate%d" % c) for c in range(CHUNKS)]
        z = keep.tile([P, S, PACK], BF16, align_bytes=64)
        z_q = keep.tile([P, S], U32, align_bytes=64)
        z_s = keep.tile([P, S], U8, align_bytes=64)
        yb = keep.tile([P, S, PACK], BF16, align_bytes=64)
        y_q = keep.tile([P, S], U32, align_bytes=64)
        y = [keep.tile([P, PACK, CHUNK], F32, name="y%d" % c) for c in range(CHUNKS)]

        def quantize(codes, scales, values, cols):
            nc.vector.quantize_mx(
                out=codes[:, cols].bitcast(FP8X4), scales=scales[:, cols], in_=values[:, cols, :].rearrange("p j t -> p (j t)")
            )

        def second(c):
            cols = slice(c * CHUNK, (c + 1) * CHUNK)
            bank = psum.tile([P, PACK, CHUNK], F32, name="g_bank%d" % c)
            for t in range(PACK):
                m = slice(t * P, (t + 1) * P)
                nc.tensor.matmul_mx(
                    out=bank[:, t, :],
                    lhsT=d_q[:, m].bitcast(FP8X4),
                    lhsT_scale=d_s[:, m],
                    rhs=z_q[:, cols].bitcast(FP8X4),
                    rhs_scale=z_s[:, cols],
                    start=True,
                    stop=True,
                )
            nc.scalar.activation(gate[c][:], bank[:], TANH, scale=0.03125)

        def finish(c):
            b, lo = divmod(c * CHUNK, HALF)
            cols = slice(c * CHUNK, (c + 1) * CHUNK)
            nc.vector.scalar_tensor_tensor(y[c][:], gate[c][:], 1.0, own[b][:, :, lo : lo + CHUNK], ADD, MULT)
            nc.sync.dma_start(out_rows[:, :, cols], y[c][:])

        def weave(c, copy):
            copy(yb[:, c * CHUNK : (c + 1) * CHUNK, :], y[c][:].rearrange("p t j -> p j t"))

        def emit(b):
            cols = slice(b * HALF, (b + 1) * HALF)
            quantize(y_q, o_s, yb, cols)
            nc.sync.dma_start(out_words[:, cols], y_q[:, cols].bitcast(I32))

        for t in range(PACK):
            nc.scalar.activation(window[t][:], h_bank[t][:], COPY, scale=0.5)
            nc.scalar.activation(own[0][:, t, :], h_bank[t][:, 0:HALF], COPY, scale=0.5)
            nc.sync.dma_start(own[1][:, t, :], window[t][:, HALF:S])
            gather(0, t)
        first_th = keep.tile([P, PACK, HALF], F32)
        first_z = keep.tile([P, PACK, HALF], BF16)
        nc.scalar.activation(first_th[:], pre[0][:], TANH, scale=2.0)
        for t in range(PACK):
            gather(1, t)
            nc.scalar.activation(first_z[:, t, :], first_th[:, t, :], COPY, scale=gain[:, t : t + 1])
        nc.vector.tensor_copy(z[:, 0:HALF, :], first_z[:].rearrange("p t j -> p j t"))
        quantize(z_q, z_s, z, slice(0, HALF))
        th = [keep.tile([P, CHUNK, PACK], F32, name="th%d" % u) for u in range(2)]
        for u in range(2):
            sums = pre[1][:, :, u * CHUNK : (u + 1) * CHUNK]
            nc.scalar.activation(th[u][:], sums.rearrange("p t j -> p j t"), TANH, scale=2.0)
        for u in range(2):
            cols = slice(HALF + u * CHUNK, HALF + (u + 1) * CHUNK)
            nc.vector.tensor_tensor(z[:, cols, :], th[u][:], gain[:].unsqueeze(1).to_broadcast([P, CHUNK, PACK]), MULT)
        second(0)
        second(1)
        for u in range(2):
            quantize(z_q, z_s, z, slice(HALF + u * CHUNK, HALF + (u + 1) * CHUNK))
        second(2)
        second(3)
        for c in range(CHUNKS):
            finish(c)
        weave(0, nc.scalar.copy)
        weave(1, nc.scalar.copy)
        weave(2, nc.vector.tensor_copy)
        weave(3, nc.vector.tensor_copy)
        emit(0)
        emit(1)
        for r in range(4):
            queue = nc.sync if r % 2 else nc.scalar
            queue.dma_start(out_2[0, r:16:4, :].bitcast(I32), o_s[r:P:32, :].bitcast(I32))
